import numpy as np
import ml_dtypes


def mxq(x, axis, fmt="e4m3"):
    dtype, down = {"e4m3": (ml_dtypes.float8_e4m3fn, 7), "e5m2": (ml_dtypes.float8_e5m2, 14)}[fmt]
    v = np.moveaxis(np.asarray(x, np.float32).astype(ml_dtypes.bfloat16).astype(np.float64), axis, -1)
    blocks = v.reshape(v.shape[:-1] + (-1, 32))
    amax = np.abs(blocks).max(-1, keepdims=True)
    byte = np.maximum(np.where(amax > 0, np.frexp(amax)[1] - 1 + 127, 0) - down, 1)
    scale = np.exp2(byte - 127.0)
    codes = (blocks / scale).astype(np.float32).astype(dtype).astype(np.float64)
    return np.moveaxis((codes * scale).reshape(v.shape), -1, axis)


WIDE = False


def mx_kscale(k):
    if not WIDE:
        return np.ones(k)
    levels = np.array([10, -10, 5, -5, 0])
    if k % 512:
        return np.exp2(np.random.permutation(np.resize(levels, k // 32))).repeat(32)
    a = np.empty((k // 512, 16))
    for p in range(k // 512):
        a[p, :8] = np.random.permutation(np.resize(levels, 8))
        for g in range(8):
            far = levels[np.abs(levels - a[p, g]) >= 10]
            a[p, g + 8] = far[np.random.randint(len(far))]
    return np.exp2(a.ravel()).repeat(32)


BF16 = ml_dtypes.bfloat16


def bf(x):
    return np.asarray(x, np.float32).astype(BF16)


def f64(x):
    return np.asarray(x).astype(np.float64)

E4M3FN = np.array([(-1.0 if i & 128 else 1.0) * ((1.0 + (i & 7) / 8.0) * 2.0 ** (((i >> 3) & 15) - 7) if i & 120 else (i & 7) * 2.0 ** -9) for i in range(256)])


def e4m3fn_bytes(y):
    return np.clip(np.asarray(y, np.float64), -448.0, 448.0).astype(np.float32).astype(ml_dtypes.float8_e4m3fn).view(np.uint8)


def e4m3fn_values(b):
    return E4M3FN[b]


T, K, N, B = 2048, 1536, 1024, 128


def setup_inputs():
    f = mx_kscale(K)
    ret = np.random.standard_normal((T, K)) * f
    ret_scale = (np.abs(ret.reshape(T, K // B, B)).max(axis=2) / 448.0).astype(np.float32)
    ret_bytes = e4m3fn_bytes(ret / np.repeat(f64(ret_scale), B, axis=1))
    size = np.random.uniform(0.5, 1.5, (N, 1))
    pos = size * np.random.standard_normal((N, K)) / np.sqrt(K) / f
    rate = np.random.uniform(0.2, 1.0, K) / np.sqrt(K) * f
    return {"ret_bytes": ret_bytes,
            "ret_scale": ret_scale,
            "pos": bf(pos),
            "rate": bf(rate)}


def reference(ret_bytes, ret_scale, pos, rate):
    ret = e4m3fn_values(ret_bytes) * np.repeat(f64(ret_scale), B, axis=1)
    p = f64(pos)
    gross = mxq(ret, 1, "e4m3") @ mxq(p, 1, "e4m3").T
    cost = (np.abs(p) * f64(rate)).sum(axis=1)
    return gross - cost

@@ -1,0 +1,287 @@
+from contextlib import ExitStack
+
+import concourse.mybir as mybir
+from concourse.masks import make_identity
+
+T, K, N = 2048, 1536, 1024
+FLOPS = 2 * T * K * N + 3 * N * K
+
+F32 = mybir.dt.float32
+BF16 = mybir.dt.bfloat16
+U32 = mybir.dt.uint32
+I32 = mybir.dt.int32
+U8 = mybir.dt.uint8
+FP8 = mybir.dt.float8_e4m3fn
+FP8X4 = mybir.dt.float8_e4m3fn_x4
+ALU = mybir.AluOpType
+COPY = mybir.ActivationFunctionType.Copy
+
+P = 128
+G = K // 512
+BLOCKS = K // 128
+TILES = T // P
+PAIRS = TILES // 2
+POS_PAIRS = N // 256
+MANUAL = True
+
+
+def tile_scenario_profit_after_cost_d1_kernel(tc, ret_bytes, ret_scale, pos, rate, out):
+    nc = tc.nc
+    with ExitStack() as ctx:
+        const = ctx.enter_context(tc.tile_pool(name="const", bufs=1))
+        work = ctx.enter_context(tc.tile_pool(name="work", bufs=3))
+        psum = ctx.enter_context(tc.psum_pool(name="psum", bufs=4))
+        if MANUAL:
+            ctx.enter_context(tc.manual_schedule())
+
+        ident = const.tile([P, P], F32, name="ident")
+        make_identity(nc, ident[:])
+
+        bytes_v = ret_bytes.rearrange("(p i) k -> p i k", i=TILES)
+        out_v = out.rearrange("(p i) n -> p i n", i=TILES)
+        pos_v = pos.rearrange("(c s r) k -> c r s k", s=2, r=P)
+
+        rate_sb = const.tile([P, G, 4], BF16, name="rate_sb")
+        scale_sb = const.tile([P, TILES, BLOCKS], F32, name="scale_sb")
+        pos_sb = [const.tile([P, 2, K], BF16, name=f"pos_sb{c}", align_bytes=64) for c in range(POS_PAIRS)]
+        ret_u8 = [const.tile([P, 2, K], U8, name=f"ret_u8_{i}", align_bytes=64) for i in range(PAIRS)]
+
+        nc.scalar.dma_start(out=scale_sb[:], in_=ret_scale.rearrange("(p i) b -> p i b", i=TILES))
+        nc.scalar.dma_start(out=rate_sb[:], in_=rate.rearrange("(g p t) -> p g t", p=P, t=4))
+        for g in range(G):
+            nc.sync.dma_start(out=pos_sb[0][:, :, 512 * g : 512 * g + 512], in_=pos_v[0][:, :, 512 * g : 512 * g + 512])
+        nc.sync.dma_start(out=ret_u8[0][:], in_=bytes_v[:, 0:2, :])
+        for c in range(1, POS_PAIRS):
+            nc.sync.dma_start(out=pos_sb[c][:], in_=pos_v[c])
+        for i in range(1, PAIRS):
+            nc.sync.dma_start(out=ret_u8[i][:], in_=bytes_v[:, 2 * i : 2 * i + 2, :])
+
+        pos_q = const.tile([P, G, N], U32, name="pos_q", align_bytes=64)
+        pos_s = const.tile([P, G, N], U8, name="pos_s", align_bytes=64)
+        pos_abs = const.tile([P, POS_PAIRS, G, 2, 256], I32, name="pos_abs", align_bytes=64)
+        cost_col = const.tile([P, N // P], F32, name="cost_col")
+        cost_bc = const.tile([P, N], F32, name="cost_bc", align_bytes=64)
+
+        grouped = {}
+        banks = {}
+
+        def pos_transpose(c):
+            words = pos_sb[c][:].bitcast(F32)
+            for g in range(G):
+                bank = psum.tile([P, 2, 256], F32, name="tp", tag="tp", bufs=4)
+                for s in range(2):
+                    for u in range(2):
+                        nc.tensor.transpose(bank[:, u, P * s : P * s + P], words[:, s, 256 * g + u : 256 * g + 256 : 2], ident[:])
+                banks["pos", c, g] = bank
+
+        def copy_out(key, tag, bufs):
+            tile = work.tile([P, 256, 4], BF16, name=tag, tag=tag, bufs=bufs, align_bytes=64)
+            nc.scalar.copy(
+                out=tile[:].rearrange("p r t -> p (r t)").bitcast(F32).rearrange("p (r u) -> p r u", u=2),
+                in_=banks[key][:].rearrange("p u r -> p r u"),
+            )
+            grouped[key] = tile
+
+        def pos_copy(c):
+            for g in range(G):
+                copy_out(("pos", c, g), "pos_grp", 6)
+
+        def pos_quantize(c, g):
+            cols = slice(256 * c, 256 * c + 256)
+            nc.vector.quantize_mx(
+                out=pos_q[:, g, cols].bitcast(FP8X4),
+                scales=pos_s[:, g, cols],
+                in_=grouped["pos", c, g][:].rearrange("p r t -> p (r t)"),
+            )
+
+        def pos_absolute(c, g):
+            nc.vector.tensor_scalar(
+                out=pos_abs[:, c, g],
+                in0=grouped["pos", c, g][:].rearrange("p r t -> p (r t)").bitcast(I32).rearrange("p (r u) -> p u r", u=2),
+                scalar1=0x7FFF7FFF,
+                scalar2=None,
+                op0=ALU.bitwise_and,
+            )
+
+        cost_ps = {}
+
+        def cost_sum(c):
+            if c == 0:
+                cost_ps[0] = psum.tile([P, N // P], F32, name="cost_ps", tag="tp", bufs=4)
+            for s in range(2):
+                for k in range(4 * G):
+                    g, t = k // 4, k % 4
+                    u, e = t // 2, t % 2
+                    mags = pos_abs[:, c, g, u].bitcast(BF16)
+                    nc.tensor.matmul(
+                        out=cost_ps[0][:, 2 * c + s : 2 * c + s + 1],
+                        lhsT=mags[:, 256 * s + e : 256 * s + 256 : 2],
+                        rhs=rate_sb[:, g, t : t + 1],
+                        start=(k == 0),
+                        stop=(k == 4 * G - 1),
+                    )
+
+        def cost_spread_tensor():
+            for h in range(2):
+                bank = psum.tile([P, 512], F32, name="tp", tag="tp", bufs=4)
+                for m in range(4):
+                    col = 4 * h + m
+                    nc.tensor.transpose(bank[:, P * m : P * m + P], cost_col[:, col : col + 1].to_broadcast([P, P]), ident[:])
+                banks["cost", h] = bank
+
+        def cost_spread_copy():
+            for h in range(2):
+                nc.scalar.copy(out=cost_bc[:, 512 * h : 512 * h + 512], in_=banks["cost", h][:])
+
+        wide = {}
+
+        def new_wide(i):
+            wide[i, 0] = work.tile([P, K], BF16, name="wide_a", tag="wide_a", bufs=3, align_bytes=64)
+            wide[i, 1] = work.tile([P, K], BF16, name="wide_b", tag="wide_b", bufs=3, align_bytes=64)
+
+        def widen_a(i, first, last):
+            dst = wide[i, 0][:].rearrange("r (g u p e) -> r g p u e", g=G, u=2, e=2)
+            for b in range(first, last):
+                q = b % 4
+                nc.vector.tensor_scalar(
+                    out=dst[:, b // 4, 32 * q : 32 * q + 32],
+                    in0=ret_u8[i][:, 0, P * b : P * b + P].bitcast(FP8).rearrange("r (p u e) -> r p u e", u=2, e=2),
+                    scalar1=scale_sb[:, 2 * i, b : b + 1],
+                    scalar2=None,
+                    op0=ALU.mult,
+                )
+
+        def widen_b(i):
+            for b in range(BLOCKS):
+                nc.scalar.activation(
+                    out=wide[i, 1][:, P * b : P * b + P],
+                    in_=ret_u8[i][:, 1, P * b : P * b + P].bitcast(FP8),
+                    func=COPY,
+                    scale=scale_sb[:, 2 * i + 1, b : b + 1],
+                )
+
+        def ret_transpose(i):
+            words_a = wide[i, 0][:].bitcast(F32)
+            words_b = wide[i, 1][:].bitcast(F32)
+            for g in range(G):
+                bank = psum.tile([P, 2, 256], F32, name="tp", tag="tp", bufs=4)
+                for u in range(2):
+                    nc.tensor.transpose(bank[:, u, 0:P], words_a[:, 256 * g + P * u : 256 * g + P * u + P], ident[:])
+                for u in range(2):
+                    nc.tensor.transpose(bank[:, u, P : 2 * P], words_b[:, 256 * g + u : 256 * g + 256 : 2], ident[:])
+                banks["ret", i, g] = bank
+
+        def ret_copy(i):
+            for g in range(G):
+                copy_out(("ret", i, g), "ret_grp", 6)
+
+        ret_q = {}
+        ret_s = {}
+
+        def new_ret_q(i):
+            ret_q[i] = work.tile([P, G, 256], U32, name="ret_q", tag="ret_q", bufs=3, align_bytes=64)
+            ret_s[i] = work.tile([P, G, 256], U8, name="ret_s", tag="ret_s", bufs=3, align_bytes=64)
+
+        def ret_quantize(i, g):
+            nc.vector.quantize_mx(
+                out=ret_q[i][:, g].bitcast(FP8X4),
+                scales=ret_s[i][:, g],
+                in_=grouped["ret", i, g][:].rearrange("p r t -> p (r t)"),
+            )
+
+        sums = {}
+
+        def product(i, s, h):
+            acc = psum.tile([P, 512], F32, name="mx", tag="mx", bufs=4)
+            for g in range(G):
+                nc.tensor.matmul_mx(
+                    out=acc[:],
+                    lhsT=ret_q[i][:, g, P * s : P * s + P].bitcast(FP8X4),
+                    lhsT_scale=ret_s[i][:, g, P * s : P * s + P],
+                    rhs=pos_q[:, g, 512 * h : 512 * h + 512].bitcast(FP8X4),
+                    rhs_scale=pos_s[:, g, 512 * h : 512 * h + 512],
+                    start=(g == 0),
+                    stop=(g == G - 1),
+                )
+            sums[i, s, h] = acc
+
+        result = {}
+
+        def finish(i, s, h):
+            if h == 0:
+                result[i, s] = work.tile([P, N], F32, name="res", tag="res", bufs=6, align_bytes=64)
+            cols = slice(512 * h, 512 * h + 512)
+            nc.vector.tensor_tensor(out=result[i, s][:, cols], in0=sums[i, s, h][:], in1=cost_bc[:, cols], op=ALU.subtract)
+            if i == PAIRS - 1 and s == 1:
+                nc.sync.dma_start(out=out_v[:, 2 * i + s, cols], in_=result[i, s][:, cols])
+            elif h == 1:
+                nc.sync.dma_start(out=out_v[:, 2 * i + s, :], in_=result[i, s][:])
+
+        pos_transpose(0)
+        pos_copy(0)
+        new_wide(0)
+        widen_a(0, 0, BLOCKS)
+        for g in range(G):
+            pos_quantize(0, g)
+            pos_absolute(0, g)
+        widen_b(0)
+        pos_transpose(1)
+        pos_copy(1)
+        ret_transpose(0)
+        ret_copy(0)
+        for g in range(G):
+            pos_quantize(1, g)
+            pos_absolute(1, g)
+        new_ret_q(0)
+        for g in range(G):
+            ret_quantize(0, g)
+        pos_transpose(2)
+        pos_copy(2)
+        for g in range(G):
+            pos_quantize(2, g)
+            pos_absolute(2, g)
+        pos_transpose(3)
+        pos_copy(3)
+        new_wide(1)
+        widen_a(1, 0, BLOCKS)
+        for g in range(G):
+            pos_absolute(3, g)
+            pos_quantize(3, g)
+        widen_b(1)
+        product(0, 0, 0)
+        product(0, 1, 0)
+        for c in range(POS_PAIRS):
+            cost_sum(c)
+        nc.vector.tensor_copy(out=cost_col[:], in_=cost_ps[0][:])
+        product(0, 0, 1)
+        product(0, 1, 1)
+        cost_spread_tensor()
+        cost_spread_copy()
+
+        for i in range(PAIRS):
+            nxt, far = i + 1, i + 2
+            if nxt < PAIRS:
+                ret_transpose(nxt)
+            if i > 0:
+                finish(i - 1, 1, 1)
+            if nxt < PAIRS:
+                ret_copy(nxt)
+                new_ret_q(nxt)
+            if far < PAIRS:
+                new_wide(far)
+                widen_a(far, 0, 6)
+            for g in range(G):
+                if nxt < PAIRS:
+                    ret_quantize(nxt, g)
+                if far < PAIRS:
+                    widen_a(far, 6 + 2 * g, 8 + 2 * g)
+            if far < PAIRS:
+                widen_b(far)
+            if i > 0:
+                for s in range(2):
+                    for h in range(2):
+                        product(i, s, h)
+            finish(i, 0, 0)
+            finish(i, 0, 1)
+            finish(i, 1, 0)
+        finish(PAIRS - 1, 1, 1)

@@ -23,6 +23,7 @@ TILES = T // P
 PAIRS = TILES // 2
 POS_PAIRS = N // 256
 MANUAL = True
+PERM_FROM = 4
 
 
 def tile_scenario_profit_after_cost_d1_kernel(tc, ret_bytes, ret_scale, pos, rate, out):
@@ -39,7 +40,6 @@ def tile_scenario_profit_after_cost_d1_kernel(tc, ret_bytes, ret_scale, pos, rat
 
         bytes_v = ret_bytes.rearrange("(p i) k -> p i k", i=TILES)
         out_v = out.rearrange("(p i) n -> p i n", i=TILES)
-        pos_v = pos.rearrange("(c s r) k -> c r s k", s=2, r=P)
 
         rate_sb = const.tile([P, G, 4], BF16, name="rate_sb")
         scale_sb = const.tile([P, TILES, BLOCKS], F32, name="scale_sb")
@@ -48,13 +48,27 @@ def tile_scenario_profit_after_cost_d1_kernel(tc, ret_bytes, ret_scale, pos, rat
 
         nc.scalar.dma_start(out=scale_sb[:], in_=ret_scale.rearrange("(p i) b -> p i b", i=TILES))
         nc.scalar.dma_start(out=rate_sb[:], in_=rate.rearrange("(g p t) -> p g t", p=P, t=4))
-        for g in range(G):
-            nc.sync.dma_start(out=pos_sb[0][:, :, 512 * g : 512 * g + 512], in_=pos_v[0][:, :, 512 * g : 512 * g + 512])
-        nc.sync.dma_start(out=ret_u8[0][:], in_=bytes_v[:, 0:2, :])
-        for c in range(1, POS_PAIRS):
-            nc.sync.dma_start(out=pos_sb[c][:], in_=pos_v[c])
-        for i in range(1, PAIRS):
+        pos_tile_v = pos.rearrange("(c s r) k -> c s r k", s=2, r=P)
+
+        def load_pos(c):
+            for s in range(2):
+                if c == 0 and s == 0:
+                    for g in range(G):
+                        cols = slice(512 * g, 512 * g + 512)
+                        nc.sync.dma_start(out=pos_sb[c][:, s, cols], in_=pos_tile_v[c, s][:, cols])
+                else:
+                    nc.sync.dma_start(out=pos_sb[c][:, s], in_=pos_tile_v[c, s])
+
+        def load_ret(i):
             nc.sync.dma_start(out=ret_u8[i][:], in_=bytes_v[:, 2 * i : 2 * i + 2, :])
+
+        load_pos(0)
+        load_pos(1)
+        load_ret(0)
+        load_pos(2)
+        load_pos(3)
+        for i in range(1, PAIRS):
+            load_ret(i)
 
         pos_q = const.tile([P, G, N], U32, name="pos_q", align_bytes=64)
         pos_s = const.tile([P, G, N], U8, name="pos_s", align_bytes=64)
@@ -68,11 +82,14 @@ def tile_scenario_profit_after_cost_d1_kernel(tc, ret_bytes, ret_scale, pos, rat
         def pos_transpose(c):
             words = pos_sb[c][:].bitcast(F32)
             for g in range(G):
-                bank = psum.tile([P, 2, 256], F32, name="tp", tag="tp", bufs=4)
-                for s in range(2):
+                tag = "mx" if c % 2 else "tp"
+                banks["pos", c, g] = psum.tile([P, 2, 256], F32, name=tag, tag=tag, bufs=4)
+            for s in range(2):
+                for g in range(G):
                     for u in range(2):
-                        nc.tensor.transpose(bank[:, u, P * s : P * s + P], words[:, s, 256 * g + u : 256 * g + 256 : 2], ident[:])
-                banks["pos", c, g] = bank
+                        nc.tensor.transpose(
+                            banks["pos", c, g][:, u, P * s : P * s + P], words[:, s, 256 * g + u : 256 * g + 256 : 2], ident[:]
+                        )
 
         def copy_out(key, tag, bufs):
             tile = work.tile([P, 256, 4], BF16, name=tag, tag=tag, bufs=bufs, align_bytes=64)
@@ -82,9 +99,8 @@ def tile_scenario_profit_after_cost_d1_kernel(tc, ret_bytes, ret_scale, pos, rat
             )
             grouped[key] = tile
 
-        def pos_copy(c):
-            for g in range(G):
-                copy_out(("pos", c, g), "pos_grp", 6)
+        def pos_copy(c, g):
+            copy_out(("pos", c, g), "pos_grp", 6)
 
         def pos_quantize(c, g):
             cols = slice(256 * c, 256 * c + 256)
@@ -106,38 +122,36 @@ def tile_scenario_profit_after_cost_d1_kernel(tc, ret_bytes, ret_scale, pos, rat
         cost_ps = {}
 
         def cost_sum(c):
-            if c == 0:
-                cost_ps[0] = psum.tile([P, N // P], F32, name="cost_ps", tag="tp", bufs=4)
+            tag = "mx" if c == 1 else "tp"
+            cost_ps[c] = psum.tile([P, 2], F32, name=tag, tag=tag, bufs=4)
             for s in range(2):
                 for k in range(4 * G):
                     g, t = k // 4, k % 4
                     u, e = t // 2, t % 2
                     mags = pos_abs[:, c, g, u].bitcast(BF16)
                     nc.tensor.matmul(
-                        out=cost_ps[0][:, 2 * c + s : 2 * c + s + 1],
+                        out=cost_ps[c][:, s : s + 1],
                         lhsT=mags[:, 256 * s + e : 256 * s + 256 : 2],
                         rhs=rate_sb[:, g, t : t + 1],
                         start=(k == 0),
                         stop=(k == 4 * G - 1),
                     )
 
-        def cost_spread_tensor():
-            for h in range(2):
-                bank = psum.tile([P, 512], F32, name="tp", tag="tp", bufs=4)
-                for m in range(4):
-                    col = 4 * h + m
-                    nc.tensor.transpose(bank[:, P * m : P * m + P], cost_col[:, col : col + 1].to_broadcast([P, P]), ident[:])
-                banks["cost", h] = bank
+        def cost_spread_tensor(h):
+            bank = psum.tile([P, 512], F32, name="tp", tag="tp", bufs=4)
+            for m in range(4):
+                col = 4 * h + m
+                nc.tensor.transpose(bank[:, P * m : P * m + P], cost_col[:, col : col + 1].to_broadcast([P, P]), ident[:])
+            banks["cost", h] = bank
 
-        def cost_spread_copy():
-            for h in range(2):
-                nc.scalar.copy(out=cost_bc[:, 512 * h : 512 * h + 512], in_=banks["cost", h][:])
+        def cost_spread_copy(h):
+            nc.scalar.copy(out=cost_bc[:, 512 * h : 512 * h + 512], in_=banks["cost", h][:])
 
         wide = {}
 
         def new_wide(i):
-            wide[i, 0] = work.tile([P, K], BF16, name="wide_a", tag="wide_a", bufs=3, align_bytes=64)
-            wide[i, 1] = work.tile([P, K], BF16, name="wide_b", tag="wide_b", bufs=3, align_bytes=64)
+            wide[i, 0] = work.tile([P, K], BF16, name="wide_a", tag="wide_a", bufs=4, align_bytes=64)
+            wide[i, 1] = work.tile([P, K], BF16, name="wide_b", tag="wide_b", bufs=4, align_bytes=64)
 
         def widen_a(i, first, last):
             dst = wide[i, 0][:].rearrange("r (g u p e) -> r g p u e", g=G, u=2, e=2)
@@ -151,8 +165,8 @@ def tile_scenario_profit_after_cost_d1_kernel(tc, ret_bytes, ret_scale, pos, rat
                     op0=ALU.mult,
                 )
 
-        def widen_b(i):
-            for b in range(BLOCKS):
+        def widen_b(i, first, last):
+            for b in range(first, last):
                 nc.scalar.activation(
                     out=wide[i, 1][:, P * b : P * b + P],
                     in_=ret_u8[i][:, 1, P * b : P * b + P].bitcast(FP8),
@@ -160,20 +174,30 @@ def tile_scenario_profit_after_cost_d1_kernel(tc, ret_bytes, ret_scale, pos, rat
                     scale=scale_sb[:, 2 * i + 1, b : b + 1],
                 )
 
+        def permute_b(i):
+            perm[i] = work.tile([P, K], BF16, name="perm_b", tag="perm_b", bufs=3, align_bytes=64)
+            nc.scalar.copy(
+                out=perm[i][:].bitcast(F32).rearrange("r (g u p) -> r g u p", g=G, u=2),
+                in_=wide[i, 1][:].bitcast(F32).rearrange("r (g p u) -> r g u p", g=G, u=2),
+            )
+
+        perm = {}
+
         def ret_transpose(i):
             words_a = wide[i, 0][:].bitcast(F32)
-            words_b = wide[i, 1][:].bitcast(F32)
+            words_b = (perm[i] if i >= PERM_FROM else wide[i, 1])[:].bitcast(F32)
+            tag = "mx" if i == 0 else "tp"
             for g in range(G):
-                bank = psum.tile([P, 2, 256], F32, name="tp", tag="tp", bufs=4)
+                bank = psum.tile([P, 2, 256], F32, name=tag, tag=tag, bufs=4)
                 for u in range(2):
                     nc.tensor.transpose(bank[:, u, 0:P], words_a[:, 256 * g + P * u : 256 * g + P * u + P], ident[:])
                 for u in range(2):
-                    nc.tensor.transpose(bank[:, u, P : 2 * P], words_b[:, 256 * g + u : 256 * g + 256 : 2], ident[:])
+                    cols = slice(256 * g + P * u, 256 * g + P * u + P) if i >= PERM_FROM else slice(256 * g + u, 256 * g + 256, 2)
+                    nc.tensor.transpose(bank[:, u, P : 2 * P], words_b[:, cols], ident[:])
                 banks["ret", i, g] = bank
 
-        def ret_copy(i):
-            for g in range(G):
-                copy_out(("ret", i, g), "ret_grp", 6)
+        def ret_copy(i, g):
+            copy_out(("ret", i, g), "ret_grp", 6)
 
         ret_q = {}
         ret_s = {}
@@ -217,71 +241,130 @@ def tile_scenario_profit_after_cost_d1_kernel(tc, ret_bytes, ret_scale, pos, rat
             elif h == 1:
                 nc.sync.dma_start(out=out_v[:, 2 * i + s, :], in_=result[i, s][:])
 
+        def cost_column(c):
+            nc.vector.tensor_copy(out=cost_col[:, 2 * c : 2 * c + 2], in_=cost_ps[c][:])
+
         pos_transpose(0)
-        pos_copy(0)
-        new_wide(0)
-        widen_a(0, 0, BLOCKS)
-        for g in range(G):
-            pos_quantize(0, g)
-            pos_absolute(0, g)
-        widen_b(0)
+        pos_copy(0, 0)
+        pos_copy(0, 2)
+        pos_copy(0, 1)
         pos_transpose(1)
-        pos_copy(1)
-        ret_transpose(0)
-        ret_copy(0)
-        for g in range(G):
-            pos_quantize(1, g)
-            pos_absolute(1, g)
-        new_ret_q(0)
-        for g in range(G):
-            ret_quantize(0, g)
         pos_transpose(2)
-        pos_copy(2)
-        for g in range(G):
-            pos_quantize(2, g)
-            pos_absolute(2, g)
+        pos_absolute(0, 0)
+        pos_copy(1, 0)
+        pos_copy(1, 2)
+        pos_quantize(0, 0)
+        pos_absolute(0, 1)
+        new_wide(0)
+        widen_a(0, 0, 6)
+        pos_absolute(1, 0)
+        widen_a(0, 6, 12)
+        widen_b(0, 0, 6)
+        widen_b(0, 6, 12)
+        pos_absolute(0, 2)
+        pos_absolute(1, 2)
+        pos_copy(2, 0)
+        pos_copy(1, 1)
+        cost_sum(0)
+        pos_copy(2, 2)
+        ret_transpose(0)
+        pos_quantize(0, 2)
+        ret_copy(0, 0)
+        new_ret_q(0)
+        pos_quantize(0, 1)
+        pos_absolute(1, 1)
+        pos_quantize(1, 0)
+        cost_sum(1)
+        ret_copy(0, 1)
+        ret_quantize(0, 0)
         pos_transpose(3)
-        pos_copy(3)
+        ret_copy(0, 2)
+        pos_quantize(2, 0)
+        cost_column(0)
+        pos_absolute(2, 2)
+        pos_copy(2, 1)
+        cost_column(1)
+        ret_quantize(0, 1)
+        cost_spread_tensor(0)
         new_wide(1)
-        widen_a(1, 0, BLOCKS)
-        for g in range(G):
-            pos_absolute(3, g)
-            pos_quantize(3, g)
-        widen_b(1)
+        pos_absolute(2, 0)
+        pos_absolute(2, 1)
+        pos_copy(3, 0)
+        pos_copy(3, 2)
+        pos_copy(3, 1)
+        pos_quantize(2, 2)
+        pos_quantize(1, 2)
+        ret_quantize(0, 2)
+        pos_quantize(1, 1)
+        widen_b(1, 0, 6)
+        pos_quantize(2, 1)
+        pos_absolute(3, 0)
+        pos_quantize(3, 0)
+        cost_sum(2)
+        pos_quantize(3, 1)
+        pos_absolute(3, 1)
+        pos_quantize(3, 2)
         product(0, 0, 0)
+        cost_column(2)
+        widen_b(1, 6, 12)
+        new_wide(2)
+        widen_a(1, 0, 6)
+        cost_spread_copy(0)
         product(0, 1, 0)
-        for c in range(POS_PAIRS):
-            cost_sum(c)
-        nc.vector.tensor_copy(out=cost_col[:], in_=cost_ps[0][:])
+        widen_a(1, 6, 12)
         product(0, 0, 1)
         product(0, 1, 1)
-        cost_spread_tensor()
-        cost_spread_copy()
+        widen_b(2, 0, 6)
+        pos_absolute(3, 2)
+        new_ret_q(1)
+        widen_a(2, 0, 6)
+        cost_sum(3)
+        cost_column(3)
+        ret_transpose(1)
+        widen_b(2, 6, 12)
+        finish(0, 0, 0)
+        widen_a(2, 6, 12)
+        ret_copy(1, 0)
+        ret_copy(1, 1)
+        finish(0, 1, 0)
+        ret_quantize(1, 0)
+        cost_spread_tensor(1)
+        ret_copy(1, 2)
+        ret_quantize(1, 2)
+        ret_transpose(2)
+        ret_quantize(1, 1)
+        cost_spread_copy(1)
+        ret_copy(2, 1)
+        ret_copy(2, 2)
+        finish(0, 1, 1)
+        ret_copy(2, 0)
+        finish(0, 0, 1)
 
-        for i in range(PAIRS):
-            nxt, far = i + 1, i + 2
-            if nxt < PAIRS:
-                ret_transpose(nxt)
-            if i > 0:
-                finish(i - 1, 1, 1)
-            if nxt < PAIRS:
-                ret_copy(nxt)
-                new_ret_q(nxt)
+        for i in range(1, PAIRS):
+            far = i + 2
+            if i + 1 < PAIRS:
+                new_ret_q(i + 1)
+                for g in range(G):
+                    ret_quantize(i + 1, g)
+            if i == 1:
+                new_wide(3)
+                widen_b(3, 0, BLOCKS)
+                if 3 >= PERM_FROM:
+                    permute_b(3)
+                widen_a(3, 0, BLOCKS)
+            for s in range(2):
+                for h in range(2):
+                    product(i, s, h)
+                    finish(i, s, h)
             if far < PAIRS:
-                new_wide(far)
-                widen_a(far, 0, 6)
-            for g in range(G):
-                if nxt < PAIRS:
-                    ret_quantize(nxt, g)
-                if far < PAIRS:
-                    widen_a(far, 6 + 2 * g, 8 + 2 * g)
-            if far < PAIRS:
-                widen_b(far)
-            if i > 0:
-                for s in range(2):
-                    for h in range(2):
-                        product(i, s, h)
-            finish(i, 0, 0)
-            finish(i, 0, 1)
-            finish(i, 1, 0)
-        finish(PAIRS - 1, 1, 1)
+                ret_transpose(far)
+                if far + 1 < PAIRS:
+                    new_wide(far + 1)
+                    widen_b(far + 1, 0, 8)
+                for g in range(G):
+                    ret_copy(far, g)
+                if far + 1 < PAIRS:
+                    widen_b(far + 1, 8, 12)
+                    if far + 1 >= PERM_FROM:
+                        permute_b(far + 1)
+                    widen_a(far + 1, 0, BLOCKS)

@@ -23,7 +23,7 @@ TILES = T // P
 PAIRS = TILES // 2
 POS_PAIRS = N // 256
 MANUAL = True
-PERM_FROM = 4
+PERM_FROM = 2
 
 
 def tile_scenario_profit_after_cost_d1_kernel(tc, ret_bytes, ret_scale, pos, rate, out):
@@ -50,25 +50,17 @@ def tile_scenario_profit_after_cost_d1_kernel(tc, ret_bytes, ret_scale, pos, rat
         nc.scalar.dma_start(out=rate_sb[:], in_=rate.rearrange("(g p t) -> p g t", p=P, t=4))
         pos_tile_v = pos.rearrange("(c s r) k -> c s r k", s=2, r=P)
 
-        def load_pos(c):
-            for s in range(2):
-                if c == 0 and s == 0:
-                    for g in range(G):
-                        cols = slice(512 * g, 512 * g + 512)
-                        nc.sync.dma_start(out=pos_sb[c][:, s, cols], in_=pos_tile_v[c, s][:, cols])
-                else:
-                    nc.sync.dma_start(out=pos_sb[c][:, s], in_=pos_tile_v[c, s])
+        def load_pos(c, s):
+            if c == 0 and s == 0:
+                for g in range(G):
+                    cols = slice(512 * g, 512 * g + 512)
+                    nc.sync.dma_start(out=pos_sb[c][:, s, cols], in_=pos_tile_v[c, s][:, cols])
+            else:
+                nc.sync.dma_start(out=pos_sb[c][:, s], in_=pos_tile_v[c, s])
 
         def load_ret(i):
             nc.sync.dma_start(out=ret_u8[i][:], in_=bytes_v[:, 2 * i : 2 * i + 2, :])
 
-        load_pos(0)
-        load_pos(1)
-        load_ret(0)
-        load_pos(2)
-        load_pos(3)
-        for i in range(1, PAIRS):
-            load_ret(i)
 
         pos_q = const.tile([P, G, N], U32, name="pos_q", align_bytes=64)
         pos_s = const.tile([P, G, N], U8, name="pos_s", align_bytes=64)
@@ -79,21 +71,20 @@ def tile_scenario_profit_after_cost_d1_kernel(tc, ret_bytes, ret_scale, pos, rat
         grouped = {}
         banks = {}
 
-        def pos_transpose(c):
+        def pos_transpose(c, s, tag):
             words = pos_sb[c][:].bitcast(F32)
-            for g in range(G):
-                tag = "mx" if c % 2 else "tp"
-                banks["pos", c, g] = psum.tile([P, 2, 256], F32, name=tag, tag=tag, bufs=4)
-            for s in range(2):
+            if s == 0:
                 for g in range(G):
-                    for u in range(2):
-                        nc.tensor.transpose(
-                            banks["pos", c, g][:, u, P * s : P * s + P], words[:, s, 256 * g + u : 256 * g + 256 : 2], ident[:]
-                        )
+                    banks["pos", c, g] = psum.tile([P, 2, 256], F32, name=tag, tag=tag, bufs=4)
+            for g in range(G):
+                for u in range(2):
+                    nc.tensor.transpose(
+                        banks["pos", c, g][:, u, P * s : P * s + P], words[:, s, 256 * g + u : 256 * g + 256 : 2], ident[:]
+                    )
 
-        def copy_out(key, tag, bufs):
+        def copy_out(key, tag, bufs, copy=None):
             tile = work.tile([P, 256, 4], BF16, name=tag, tag=tag, bufs=bufs, align_bytes=64)
-            nc.scalar.copy(
+            (copy or nc.scalar.copy)(
                 out=tile[:].rearrange("p r t -> p (r t)").bitcast(F32).rearrange("p (r u) -> p r u", u=2),
                 in_=banks[key][:].rearrange("p u r -> p r u"),
             )
@@ -101,6 +92,9 @@ def tile_scenario_profit_after_cost_d1_kernel(tc, ret_bytes, ret_scale, pos, rat
 
         def pos_copy(c, g):
             copy_out(("pos", c, g), "pos_grp", 6)
+
+        def pos_copy_v(c, g):
+            copy_out(("pos", c, g), "pos_grp", 6, nc.vector.tensor_copy)
 
         def pos_quantize(c, g):
             cols = slice(256 * c, 256 * c + 256)
@@ -121,8 +115,7 @@ def tile_scenario_profit_after_cost_d1_kernel(tc, ret_bytes, ret_scale, pos, rat
 
         cost_ps = {}
 
-        def cost_sum(c):
-            tag = "mx" if c == 1 else "tp"
+        def cost_sum(c, tag):
             cost_ps[c] = psum.tile([P, 2], F32, name=tag, tag=tag, bufs=4)
             for s in range(2):
                 for k in range(4 * G):
@@ -137,8 +130,8 @@ def tile_scenario_profit_after_cost_d1_kernel(tc, ret_bytes, ret_scale, pos, rat
                         stop=(k == 4 * G - 1),
                     )
 
-        def cost_spread_tensor(h):
-            bank = psum.tile([P, 512], F32, name="tp", tag="tp", bufs=4)
+        def cost_spread_tensor(h, tag):
+            bank = psum.tile([P, 512], F32, name=tag, tag=tag, bufs=4)
             for m in range(4):
                 col = 4 * h + m
                 nc.tensor.transpose(bank[:, P * m : P * m + P], cost_col[:, col : col + 1].to_broadcast([P, P]), ident[:])
@@ -150,6 +143,8 @@ def tile_scenario_profit_after_cost_d1_kernel(tc, ret_bytes, ret_scale, pos, rat
         wide = {}
 
         def new_wide(i):
+            if (i, 0) in wide:
+                return
             wide[i, 0] = work.tile([P, K], BF16, name="wide_a", tag="wide_a", bufs=4, align_bytes=64)
             wide[i, 1] = work.tile([P, K], BF16, name="wide_b", tag="wide_b", bufs=4, align_bytes=64)
 
@@ -174,6 +169,16 @@ def tile_scenario_profit_after_cost_d1_kernel(tc, ret_bytes, ret_scale, pos, rat
                     scale=scale_sb[:, 2 * i + 1, b : b + 1],
                 )
 
+        def widen_b_v(i, first, last):
+            for b in range(first, last):
+                nc.vector.tensor_scalar(
+                    out=wide[i, 1][:, P * b : P * b + P],
+                    in0=ret_u8[i][:, 1, P * b : P * b + P].bitcast(FP8),
+                    scalar1=scale_sb[:, 2 * i + 1, b : b + 1],
+                    scalar2=None,
+                    op0=ALU.mult,
+                )
+
         def permute_b(i):
             perm[i] = work.tile([P, K], BF16, name="perm_b", tag="perm_b", bufs=3, align_bytes=64)
             nc.scalar.copy(
@@ -183,11 +188,10 @@ def tile_scenario_profit_after_cost_d1_kernel(tc, ret_bytes, ret_scale, pos, rat
 
         perm = {}
 
-        def ret_transpose(i):
+        def ret_transpose(i, g, tag="tp"):
             words_a = wide[i, 0][:].bitcast(F32)
             words_b = (perm[i] if i >= PERM_FROM else wide[i, 1])[:].bitcast(F32)
-            tag = "mx" if i == 0 else "tp"
-            for g in range(G):
+            for g in (g,):
                 bank = psum.tile([P, 2, 256], F32, name=tag, tag=tag, bufs=4)
                 for u in range(2):
                     nc.tensor.transpose(bank[:, u, 0:P], words_a[:, 256 * g + P * u : 256 * g + P * u + P], ident[:])
@@ -198,6 +202,9 @@ def tile_scenario_profit_after_cost_d1_kernel(tc, ret_bytes, ret_scale, pos, rat
 
         def ret_copy(i, g):
             copy_out(("ret", i, g), "ret_grp", 6)
+
+        def ret_copy_v(i, g):
+            copy_out(("ret", i, g), "ret_grp", 6, nc.vector.tensor_copy)
 
         ret_q = {}
         ret_s = {}
@@ -215,156 +222,177 @@ def tile_scenario_profit_after_cost_d1_kernel(tc, ret_bytes, ret_scale, pos, rat
 
         sums = {}
 
-        def product(i, s, h):
-            acc = psum.tile([P, 512], F32, name="mx", tag="mx", bufs=4)
+        def product(i, s, h, n0=0, n=512):
+            acc = psum.tile([P, n], F32, name="mx", tag="mx", bufs=4)
             for g in range(G):
                 nc.tensor.matmul_mx(
                     out=acc[:],
                     lhsT=ret_q[i][:, g, P * s : P * s + P].bitcast(FP8X4),
                     lhsT_scale=ret_s[i][:, g, P * s : P * s + P],
-                    rhs=pos_q[:, g, 512 * h : 512 * h + 512].bitcast(FP8X4),
-                    rhs_scale=pos_s[:, g, 512 * h : 512 * h + 512],
+                    rhs=pos_q[:, g, 512 * h + n0 : 512 * h + n0 + n].bitcast(FP8X4),
+                    rhs_scale=pos_s[:, g, 512 * h + n0 : 512 * h + n0 + n],
                     start=(g == 0),
                     stop=(g == G - 1),
                 )
-            sums[i, s, h] = acc
+            sums[i, s, h, n0] = acc
 
         result = {}
 
-        def finish(i, s, h):
+        def finish(i, s, h, n0=0, n=512):
             if h == 0:
                 result[i, s] = work.tile([P, N], F32, name="res", tag="res", bufs=6, align_bytes=64)
-            cols = slice(512 * h, 512 * h + 512)
-            nc.vector.tensor_tensor(out=result[i, s][:, cols], in0=sums[i, s, h][:], in1=cost_bc[:, cols], op=ALU.subtract)
+            cols = slice(512 * h + n0, 512 * h + n0 + n)
+            nc.vector.tensor_tensor(out=result[i, s][:, cols], in0=sums[i, s, h, n0][:], in1=cost_bc[:, cols], op=ALU.subtract)
             if i == PAIRS - 1 and s == 1:
                 nc.sync.dma_start(out=out_v[:, 2 * i + s, cols], in_=result[i, s][:, cols])
-            elif h == 1:
+            elif h == 1 and n0 + n == 512:
                 nc.sync.dma_start(out=out_v[:, 2 * i + s, :], in_=result[i, s][:])
+
+        def pos_copies(c, nv):
+            for g in range(G):
+                (pos_copy_v if g >= G - nv else pos_copy)(c, g)
+
+        def ret_copies(i, nv):
+            for g in range(G):
+                (ret_copy_v if g >= G - nv else ret_copy)(i, g)
+
+        def pos_codes(c):
+            for g in range(G):
+                pos_quantize(c, g)
+
+        def pos_magnitudes(c):
+            for g in range(G):
+                pos_absolute(c, g)
+
+        def widen_a12(i):
+            new_wide(i)
+            widen_a(i, 0, BLOCKS)
+
+        def widen_b12(i, nv):
+            new_wide(i)
+            widen_b(i, 0, BLOCKS - nv)
+            widen_b_v(i, BLOCKS - nv, BLOCKS)
+            if i >= PERM_FROM:
+                permute_b(i)
+
+        def ret_transposes(i, tag):
+            for g in range(G):
+                ret_transpose(i, g, tag)
+
+        def ret_codes(i):
+            new_ret_q(i)
+            for g in range(G):
+                ret_quantize(i, g)
 
         def cost_column(c):
             nc.vector.tensor_copy(out=cost_col[:, 2 * c : 2 * c + 2], in_=cost_ps[c][:])
 
-        pos_transpose(0)
-        pos_copy(0, 0)
-        pos_copy(0, 2)
-        pos_copy(0, 1)
-        pos_transpose(1)
-        pos_transpose(2)
-        pos_absolute(0, 0)
-        pos_copy(1, 0)
-        pos_copy(1, 2)
-        pos_quantize(0, 0)
-        pos_absolute(0, 1)
-        new_wide(0)
-        widen_a(0, 0, 6)
-        pos_absolute(1, 0)
-        widen_a(0, 6, 12)
-        widen_b(0, 0, 6)
-        widen_b(0, 6, 12)
-        pos_absolute(0, 2)
-        pos_absolute(1, 2)
-        pos_copy(2, 0)
-        pos_copy(1, 1)
-        cost_sum(0)
-        pos_copy(2, 2)
-        ret_transpose(0)
-        pos_quantize(0, 2)
-        ret_copy(0, 0)
-        new_ret_q(0)
-        pos_quantize(0, 1)
-        pos_absolute(1, 1)
-        pos_quantize(1, 0)
-        cost_sum(1)
-        ret_copy(0, 1)
-        ret_quantize(0, 0)
-        pos_transpose(3)
-        ret_copy(0, 2)
-        pos_quantize(2, 0)
-        cost_column(0)
-        pos_absolute(2, 2)
-        pos_copy(2, 1)
+        load_ret(0)
+        load_pos(0, 0)
+        load_pos(0, 1)
+        load_pos(1, 0)
+        load_ret(1)
+        load_pos(1, 1)
+        load_pos(2, 0)
+        load_pos(2, 1)
+        load_pos(3, 0)
+        load_pos(3, 1)
+        load_ret(2)
+        load_ret(3)
+        load_ret(4)
+        load_ret(5)
+        load_ret(6)
+        load_ret(7)
+        widen_b12(0, 0)
+        pos_transpose(0, 0, "tp")
+        widen_a12(0)
+        pos_transpose(0, 1, "mx")
+        ret_transposes(0, "tp")
+        pos_copies(0, 1)
+        pos_transpose(1, 0, "mx")
+        pos_magnitudes(0)
+        widen_a12(1)
+        pos_codes(0)
+        pos_transpose(1, 1, "tp")
+        ret_copies(0, 0)
+        widen_b12(1, 4)
+        pos_transpose(2, 0, "tp")
+        pos_copies(1, 1)
+        pos_transpose(2, 1, "tp")
+        pos_codes(1)
+        pos_magnitudes(1)
+        ret_codes(0)
+        pos_transpose(3, 0, "mx")
+        cost_sum(0, "tp")
+        pos_transpose(3, 1, "tp")
+        pos_copies(2, 1)
+        cost_sum(1, "tp")
+        pos_copies(3, 1)
         cost_column(1)
-        ret_quantize(0, 1)
-        cost_spread_tensor(0)
-        new_wide(1)
-        pos_absolute(2, 0)
-        pos_absolute(2, 1)
-        pos_copy(3, 0)
-        pos_copy(3, 2)
-        pos_copy(3, 1)
-        pos_quantize(2, 2)
-        pos_quantize(1, 2)
-        ret_quantize(0, 2)
-        pos_quantize(1, 1)
-        widen_b(1, 0, 6)
-        pos_quantize(2, 1)
-        pos_absolute(3, 0)
-        pos_quantize(3, 0)
-        cost_sum(2)
-        pos_quantize(3, 1)
-        pos_absolute(3, 1)
-        pos_quantize(3, 2)
-        product(0, 0, 0)
-        cost_column(2)
-        widen_b(1, 6, 12)
-        new_wide(2)
-        widen_a(1, 0, 6)
+        pos_magnitudes(3)
+        cost_column(0)
+        pos_magnitudes(2)
+        ret_transposes(1, "mx")
+        cost_spread_tensor(0, "mx")
+        pos_codes(2)
+        ret_copies(1, 0)
         cost_spread_copy(0)
-        product(0, 1, 0)
-        widen_a(1, 6, 12)
+        pos_codes(3)
+        ret_codes(1)
+        cost_sum(3, "tp")
+        product(0, 0, 0)
+        widen_b12(2, 0)
+        cost_sum(2, "tp")
         product(0, 0, 1)
-        product(0, 1, 1)
-        widen_b(2, 0, 6)
-        pos_absolute(3, 2)
-        new_ret_q(1)
-        widen_a(2, 0, 6)
-        cost_sum(3)
-        cost_column(3)
-        ret_transpose(1)
-        widen_b(2, 6, 12)
+        product(1, 0, 0)
         finish(0, 0, 0)
-        widen_a(2, 6, 12)
-        ret_copy(1, 0)
-        ret_copy(1, 1)
-        finish(0, 1, 0)
-        ret_quantize(1, 0)
-        cost_spread_tensor(1)
-        ret_copy(1, 2)
-        ret_quantize(1, 2)
-        ret_transpose(2)
-        ret_quantize(1, 1)
+        cost_column(2)
+        cost_column(3)
+        product(0, 1, 0)
+        cost_spread_tensor(1, "tp")
+        widen_a12(2)
         cost_spread_copy(1)
-        ret_copy(2, 1)
-        ret_copy(2, 2)
-        finish(0, 1, 1)
-        ret_copy(2, 0)
+        finish(0, 1, 0)
+        ret_transposes(2, "tp")
+        finish(1, 0, 0)
         finish(0, 0, 1)
+        widen_a12(3)
+        product(1, 1, 0)
+        product(0, 1, 1)
+        widen_b12(3, 0)
+        product(1, 0, 1)
+        product(1, 1, 1)
+        finish(0, 1, 1)
+        finish(1, 0, 1)
+        finish(1, 1, 0)
+        ret_copies(2, 0)
+        ret_transposes(3, "tp")
+        ret_codes(2)
+        ret_copies(3, 0)
+        widen_b12(4, 4)
+        finish(1, 1, 1)
+        widen_a12(4)
 
-        for i in range(1, PAIRS):
+        for i in range(2, PAIRS):
             far = i + 2
             if i + 1 < PAIRS:
-                new_ret_q(i + 1)
-                for g in range(G):
-                    ret_quantize(i + 1, g)
-            if i == 1:
-                new_wide(3)
-                widen_b(3, 0, BLOCKS)
-                if 3 >= PERM_FROM:
-                    permute_b(3)
-                widen_a(3, 0, BLOCKS)
+                ret_codes(i + 1)
             for s in range(2):
                 for h in range(2):
-                    product(i, s, h)
-                    finish(i, s, h)
+                    if i == PAIRS - 1 and s == 1 and h == 1:
+                        for n0 in (0, 256):
+                            product(i, s, h, n0, 256)
+                            finish(i, s, h, n0, 256)
+                    else:
+                        product(i, s, h)
+                        finish(i, s, h)
             if far < PAIRS:
-                ret_transpose(far)
+                ret_transposes(far, "tp")
                 if far + 1 < PAIRS:
                     new_wide(far + 1)
                     widen_b(far + 1, 0, 8)
-                for g in range(G):
-                    ret_copy(far, g)
+                ret_copies(far, 0)
                 if far + 1 < PAIRS:
                     widen_b(far + 1, 8, 12)
-                    if far + 1 >= PERM_FROM:
-                        permute_b(far + 1)
+                    permute_b(far + 1)
                     widen_a(far + 1, 0, BLOCKS)

@@ -23,7 +23,8 @@ TILES = T // P
 PAIRS = TILES // 2
 POS_PAIRS = N // 256
 MANUAL = True
-PERM_FROM = 2
+PERM_FROM = 4
+GA = [3, 3, 3, 3, 3, 3, 3, 3]
 
 
 def tile_scenario_profit_after_cost_d1_kernel(tc, ret_bytes, ret_scale, pos, rate, out):
@@ -152,6 +153,14 @@ def tile_scenario_profit_after_cost_d1_kernel(tc, ret_bytes, ret_scale, pos, rat
             dst = wide[i, 0][:].rearrange("r (g u p e) -> r g p u e", g=G, u=2, e=2)
             for b in range(first, last):
                 q = b % 4
+                if b // 4 >= GA[i]:
+                    nc.scalar.activation(
+                        out=wide[i, 0][:, P * b : P * b + P],
+                        in_=ret_u8[i][:, 0, P * b : P * b + P].bitcast(FP8),
+                        func=COPY,
+                        scale=scale_sb[:, 2 * i, b : b + 1],
+                    )
+                    continue
                 nc.vector.tensor_scalar(
                     out=dst[:, b // 4, 32 * q : 32 * q + 32],
                     in0=ret_u8[i][:, 0, P * b : P * b + P].bitcast(FP8).rearrange("r (p u e) -> r p u e", u=2, e=2),
@@ -194,7 +203,8 @@ def tile_scenario_profit_after_cost_d1_kernel(tc, ret_bytes, ret_scale, pos, rat
             for g in (g,):
                 bank = psum.tile([P, 2, 256], F32, name=tag, tag=tag, bufs=4)
                 for u in range(2):
-                    nc.tensor.transpose(bank[:, u, 0:P], words_a[:, 256 * g + P * u : 256 * g + P * u + P], ident[:])
+                    a_cols = slice(256 * g + P * u, 256 * g + P * u + P) if g < GA[i] else slice(256 * g + u, 256 * g + 256, 2)
+                    nc.tensor.transpose(bank[:, u, 0:P], words_a[:, a_cols], ident[:])
                 for u in range(2):
                     cols = slice(256 * g + P * u, 256 * g + P * u + P) if i >= PERM_FROM else slice(256 * g + u, 256 * g + 256, 2)
                     nc.tensor.transpose(bank[:, u, P : 2 * P], words_b[:, cols], ident[:])
@@ -305,72 +315,72 @@ def tile_scenario_profit_after_cost_d1_kernel(tc, ret_bytes, ret_scale, pos, rat
         load_ret(7)
         widen_b12(0, 0)
         pos_transpose(0, 0, "tp")
-        widen_a12(0)
         pos_transpose(0, 1, "mx")
+        widen_a12(0)
         ret_transposes(0, "tp")
         pos_copies(0, 1)
-        pos_transpose(1, 0, "mx")
         pos_magnitudes(0)
-        widen_a12(1)
-        pos_codes(0)
+        pos_transpose(1, 0, "mx")
         pos_transpose(1, 1, "tp")
         ret_copies(0, 0)
-        widen_b12(1, 4)
-        pos_transpose(2, 0, "tp")
-        pos_copies(1, 1)
-        pos_transpose(2, 1, "tp")
-        pos_codes(1)
-        pos_magnitudes(1)
+        widen_a12(1)
         ret_codes(0)
-        pos_transpose(3, 0, "mx")
         cost_sum(0, "tp")
+        pos_codes(0)
+        pos_transpose(2, 0, "tp")
+        pos_transpose(3, 0, "mx")
+        pos_transpose(2, 1, "tp")
+        pos_copies(1, 0)
+        pos_magnitudes(1)
+        widen_b12(1, 0)
         pos_transpose(3, 1, "tp")
+        pos_codes(1)
+        pos_copies(3, 0)
+        cost_sum(1, "mx")
         pos_copies(2, 1)
-        cost_sum(1, "tp")
-        pos_copies(3, 1)
-        cost_column(1)
-        pos_magnitudes(3)
-        cost_column(0)
-        pos_magnitudes(2)
         ret_transposes(1, "mx")
-        cost_spread_tensor(0, "mx")
-        pos_codes(2)
-        ret_copies(1, 0)
-        cost_spread_copy(0)
-        pos_codes(3)
-        ret_codes(1)
-        cost_sum(3, "tp")
+        cost_column(0)
         product(0, 0, 0)
-        widen_b12(2, 0)
-        cost_sum(2, "tp")
-        product(0, 0, 1)
-        product(1, 0, 0)
-        finish(0, 0, 0)
-        cost_column(2)
-        cost_column(3)
+        ret_copies(1, 0)
         product(0, 1, 0)
+        cost_column(1)
+        cost_spread_tensor(0, "tp")
+        pos_magnitudes(3)
+        cost_spread_copy(0)
+        pos_codes(2)
+        cost_sum(3, "tp")
+        pos_magnitudes(2)
+        ret_codes(1)
+        cost_sum(2, "tp")
+        product(1, 0, 0)
+        pos_codes(3)
+        product(1, 1, 0)
+        finish(0, 0, 0)
+        cost_column(3)
+        product(0, 0, 1)
+        finish(0, 1, 0)
+        widen_b12(2, 0)
+        cost_column(2)
+        product(1, 0, 1)
+        widen_b12(3, 0)
         cost_spread_tensor(1, "tp")
         widen_a12(2)
-        cost_spread_copy(1)
-        finish(0, 1, 0)
         ret_transposes(2, "tp")
+        cost_spread_copy(1)
         finish(1, 0, 0)
-        finish(0, 0, 1)
         widen_a12(3)
-        product(1, 1, 0)
-        product(0, 1, 1)
-        widen_b12(3, 0)
-        product(1, 0, 1)
-        product(1, 1, 1)
-        finish(0, 1, 1)
-        finish(1, 0, 1)
+        ret_transposes(3, "tp")
+        finish(0, 0, 1)
         finish(1, 1, 0)
         ret_copies(2, 0)
-        ret_transposes(3, "tp")
+        finish(1, 0, 1)
+        product(1, 1, 1)
+        product(0, 1, 1)
         ret_codes(2)
-        ret_copies(3, 0)
-        widen_b12(4, 4)
+        widen_b12(4, 0)
         finish(1, 1, 1)
+        finish(0, 1, 1)
+        ret_copies(3, 0)
         widen_a12(4)
 
         for i in range(2, PAIRS):
@@ -394,5 +404,6 @@ def tile_scenario_profit_after_cost_d1_kernel(tc, ret_bytes, ret_scale, pos, rat
                 ret_copies(far, 0)
                 if far + 1 < PAIRS:
                     widen_b(far + 1, 8, 12)
-                    permute_b(far + 1)
+                    if far + 1 >= PERM_FROM:
+                        permute_b(far + 1)
                     widen_a(far + 1, 0, BLOCKS)

from contextlib import ExitStack

import concourse.mybir as mybir
from concourse.masks import make_identity

T, K, N = 2048, 1536, 1024
FLOPS = 2 * T * K * N + 3 * N * K

F32 = mybir.dt.float32
BF16 = mybir.dt.bfloat16
U32 = mybir.dt.uint32
I32 = mybir.dt.int32
U8 = mybir.dt.uint8
FP8 = mybir.dt.float8_e4m3fn
FP8X4 = mybir.dt.float8_e4m3fn_x4
ALU = mybir.AluOpType
COPY = mybir.ActivationFunctionType.Copy

P = 128
G = K // 512
BLOCKS = K // 128
TILES = T // P
PAIRS = TILES // 2
POS_PAIRS = N // 256
MANUAL = True
PERM_FROM = 4
GA = [3, 3, 3, 3, 3, 3, 3, 3]


def tile_scenario_profit_after_cost_d1_kernel(tc, ret_bytes, ret_scale, pos, rate, out):
    nc = tc.nc
    with ExitStack() as ctx:
        const = ctx.enter_context(tc.tile_pool(name="const", bufs=1))
        work = ctx.enter_context(tc.tile_pool(name="work", bufs=3))
        psum = ctx.enter_context(tc.psum_pool(name="psum", bufs=4))
        if MANUAL:
            ctx.enter_context(tc.manual_schedule())

        ident = const.tile([P, P], F32, name="ident")
        make_identity(nc, ident[:])

        bytes_v = ret_bytes.rearrange("(p i) k -> p i k", i=TILES)
        out_v = out.rearrange("(p i) n -> p i n", i=TILES)

        rate_sb = const.tile([P, G, 4], BF16, name="rate_sb")
        scale_sb = const.tile([P, TILES, BLOCKS], F32, name="scale_sb")
        pos_sb = [const.tile([P, 2, K], BF16, name=f"pos_sb{c}", align_bytes=64) for c in range(POS_PAIRS)]
        ret_u8 = [const.tile([P, 2, K], U8, name=f"ret_u8_{i}", align_bytes=64) for i in range(PAIRS)]

        nc.scalar.dma_start(out=scale_sb[:], in_=ret_scale.rearrange("(p i) b -> p i b", i=TILES))
        nc.scalar.dma_start(out=rate_sb[:], in_=rate.rearrange("(g p t) -> p g t", p=P, t=4))
        pos_tile_v = pos.rearrange("(c s r) k -> c s r k", s=2, r=P)

        def load_pos(c, s):
            if c == 0 and s == 0:
                for g in range(G):
                    cols = slice(512 * g, 512 * g + 512)
                    nc.sync.dma_start(out=pos_sb[c][:, s, cols], in_=pos_tile_v[c, s][:, cols])
            else:
                nc.sync.dma_start(out=pos_sb[c][:, s], in_=pos_tile_v[c, s])

        def load_ret(i):
            nc.sync.dma_start(out=ret_u8[i][:], in_=bytes_v[:, 2 * i : 2 * i + 2, :])


        pos_q = const.tile([P, G, N], U32, name="pos_q", align_bytes=64)
        pos_s = const.tile([P, G, N], U8, name="pos_s", align_bytes=64)
        pos_abs = const.tile([P, POS_PAIRS, G, 2, 256], I32, name="pos_abs", align_bytes=64)
        cost_col = const.tile([P, N // P], F32, name="cost_col")
        cost_bc = const.tile([P, N], F32, name="cost_bc", align_bytes=64)

        grouped = {}
        banks = {}

        def pos_transpose(c, s, tag):
            words = pos_sb[c][:].bitcast(F32)
            if s == 0:
                for g in range(G):
                    banks["pos", c, g] = psum.tile([P, 2, 256], F32, name=tag, tag=tag, bufs=4)
            for g in range(G):
                for u in range(2):
                    nc.tensor.transpose(
                        banks["pos", c, g][:, u, P * s : P * s + P], words[:, s, 256 * g + u : 256 * g + 256 : 2], ident[:]
                    )

        def copy_out(key, tag, bufs, copy=None):
            tile = work.tile([P, 256, 4], BF16, name=tag, tag=tag, bufs=bufs, align_bytes=64)
            (copy or nc.scalar.copy)(
                out=tile[:].rearrange("p r t -> p (r t)").bitcast(F32).rearrange("p (r u) -> p r u", u=2),
                in_=banks[key][:].rearrange("p u r -> p r u"),
            )
            grouped[key] = tile

        def pos_copy(c, g):
            copy_out(("pos", c, g), "pos_grp", 6)

        def pos_copy_v(c, g):
            copy_out(("pos", c, g), "pos_grp", 6, nc.vector.tensor_copy)

        def pos_quantize(c, g):
            cols = slice(256 * c, 256 * c + 256)
            nc.vector.quantize_mx(
                out=pos_q[:, g, cols].bitcast(FP8X4),
                scales=pos_s[:, g, cols],
                in_=grouped["pos", c, g][:].rearrange("p r t -> p (r t)"),
            )

        def pos_absolute(c, g):
            nc.vector.tensor_scalar(
                out=pos_abs[:, c, g],
                in0=grouped["pos", c, g][:].rearrange("p r t -> p (r t)").bitcast(I32).rearrange("p (r u) -> p u r", u=2),
                scalar1=0x7FFF7FFF,
                scalar2=None,
                op0=ALU.bitwise_and,
            )

        cost_ps = {}

        def cost_sum(c, tag):
            cost_ps[c] = psum.tile([P, 2], F32, name=tag, tag=tag, bufs=4)
            for s in range(2):
                for k in range(4 * G):
                    g, t = k // 4, k % 4
                    u, e = t // 2, t % 2
                    mags = pos_abs[:, c, g, u].bitcast(BF16)
                    nc.tensor.matmul(
                        out=cost_ps[c][:, s : s + 1],
                        lhsT=mags[:, 256 * s + e : 256 * s + 256 : 2],
                        rhs=rate_sb[:, g, t : t + 1],
                        start=(k == 0),
                        stop=(k == 4 * G - 1),
                    )

        def cost_spread_tensor(h, tag):
            bank = psum.tile([P, 512], F32, name=tag, tag=tag, bufs=4)
            for m in range(4):
                col = 4 * h + m
                nc.tensor.transpose(bank[:, P * m : P * m + P], cost_col[:, col : col + 1].to_broadcast([P, P]), ident[:])
            banks["cost", h] = bank

        def cost_spread_copy(h):
            nc.scalar.copy(out=cost_bc[:, 512 * h : 512 * h + 512], in_=banks["cost", h][:])

        wide = {}

        def new_wide(i):
            if (i, 0) in wide:
                return
            wide[i, 0] = work.tile([P, K], BF16, name="wide_a", tag="wide_a", bufs=4, align_bytes=64)
            wide[i, 1] = work.tile([P, K], BF16, name="wide_b", tag="wide_b", bufs=4, align_bytes=64)

        def widen_a(i, first, last):
            dst = wide[i, 0][:].rearrange("r (g u p e) -> r g p u e", g=G, u=2, e=2)
            for b in range(first, last):
                q = b % 4
                if b // 4 >= GA[i]:
                    nc.scalar.activation(
                        out=wide[i, 0][:, P * b : P * b + P],
                        in_=ret_u8[i][:, 0, P * b : P * b + P].bitcast(FP8),
                        func=COPY,
                        scale=scale_sb[:, 2 * i, b : b + 1],
                    )
                    continue
                nc.vector.tensor_scalar(
                    out=dst[:, b // 4, 32 * q : 32 * q + 32],
                    in0=ret_u8[i][:, 0, P * b : P * b + P].bitcast(FP8).rearrange("r (p u e) -> r p u e", u=2, e=2),
                    scalar1=scale_sb[:, 2 * i, b : b + 1],
                    scalar2=None,
                    op0=ALU.mult,
                )

        def widen_b(i, first, last):
            for b in range(first, last):
                nc.scalar.activation(
                    out=wide[i, 1][:, P * b : P * b + P],
                    in_=ret_u8[i][:, 1, P * b : P * b + P].bitcast(FP8),
                    func=COPY,
                    scale=scale_sb[:, 2 * i + 1, b : b + 1],
                )

        def widen_b_v(i, first, last):
            for b in range(first, last):
                nc.vector.tensor_scalar(
                    out=wide[i, 1][:, P * b : P * b + P],
                    in0=ret_u8[i][:, 1, P * b : P * b + P].bitcast(FP8),
                    scalar1=scale_sb[:, 2 * i + 1, b : b + 1],
                    scalar2=None,
                    op0=ALU.mult,
                )

        def permute_b(i):
            perm[i] = work.tile([P, K], BF16, name="perm_b", tag="perm_b", bufs=3, align_bytes=64)
            nc.scalar.copy(
                out=perm[i][:].bitcast(F32).rearrange("r (g u p) -> r g u p", g=G, u=2),
                in_=wide[i, 1][:].bitcast(F32).rearrange("r (g p u) -> r g u p", g=G, u=2),
            )

        perm = {}

        def ret_transpose(i, g, tag="tp"):
            words_a = wide[i, 0][:].bitcast(F32)
            words_b = (perm[i] if i >= PERM_FROM else wide[i, 1])[:].bitcast(F32)
            for g in (g,):
                bank = psum.tile([P, 2, 256], F32, name=tag, tag=tag, bufs=4)
                for u in range(2):
                    a_cols = slice(256 * g + P * u, 256 * g + P * u + P) if g < GA[i] else slice(256 * g + u, 256 * g + 256, 2)
                    nc.tensor.transpose(bank[:, u, 0:P], words_a[:, a_cols], ident[:])
                for u in range(2):
                    cols = slice(256 * g + P * u, 256 * g + P * u + P) if i >= PERM_FROM else slice(256 * g + u, 256 * g + 256, 2)
                    nc.tensor.transpose(bank[:, u, P : 2 * P], words_b[:, cols], ident[:])
                banks["ret", i, g] = bank

        def ret_copy(i, g):
            copy_out(("ret", i, g), "ret_grp", 6)

        def ret_copy_v(i, g):
            copy_out(("ret", i, g), "ret_grp", 6, nc.vector.tensor_copy)

        ret_q = {}
        ret_s = {}

        def new_ret_q(i):
            ret_q[i] = work.tile([P, G, 256], U32, name="ret_q", tag="ret_q", bufs=3, align_bytes=64)
            ret_s[i] = work.tile([P, G, 256], U8, name="ret_s", tag="ret_s", bufs=3, align_bytes=64)

        def ret_quantize(i, g):
            nc.vector.quantize_mx(
                out=ret_q[i][:, g].bitcast(FP8X4),
                scales=ret_s[i][:, g],
                in_=grouped["ret", i, g][:].rearrange("p r t -> p (r t)"),
            )

        sums = {}

        def product(i, s, h, n0=0, n=512):
            acc = psum.tile([P, n], F32, name="mx", tag="mx", bufs=4)
            for g in range(G):
                nc.tensor.matmul_mx(
                    out=acc[:],
                    lhsT=ret_q[i][:, g, P * s : P * s + P].bitcast(FP8X4),
                    lhsT_scale=ret_s[i][:, g, P * s : P * s + P],
                    rhs=pos_q[:, g, 512 * h + n0 : 512 * h + n0 + n].bitcast(FP8X4),
                    rhs_scale=pos_s[:, g, 512 * h + n0 : 512 * h + n0 + n],
                    start=(g == 0),
                    stop=(g == G - 1),
                )
            sums[i, s, h, n0] = acc

        result = {}

        def finish(i, s, h, n0=0, n=512):
            if h == 0:
                result[i, s] = work.tile([P, N], F32, name="res", tag="res", bufs=6, align_bytes=64)
            cols = slice(512 * h + n0, 512 * h + n0 + n)
            nc.vector.tensor_tensor(out=result[i, s][:, cols], in0=sums[i, s, h, n0][:], in1=cost_bc[:, cols], op=ALU.subtract)
            if i == PAIRS - 1 and s == 1:
                nc.sync.dma_start(out=out_v[:, 2 * i + s, cols], in_=result[i, s][:, cols])
            elif h == 1 and n0 + n == 512:
                nc.sync.dma_start(out=out_v[:, 2 * i + s, :], in_=result[i, s][:])

        def pos_copies(c, nv):
            for g in range(G):
                (pos_copy_v if g >= G - nv else pos_copy)(c, g)

        def ret_copies(i, nv):
            for g in range(G):
                (ret_copy_v if g >= G - nv else ret_copy)(i, g)

        def pos_codes(c):
            for g in range(G):
                pos_quantize(c, g)

        def pos_magnitudes(c):
            for g in range(G):
                pos_absolute(c, g)

        def widen_a12(i):
            new_wide(i)
            widen_a(i, 0, BLOCKS)

        def widen_b12(i, nv):
            new_wide(i)
            widen_b(i, 0, BLOCKS - nv)
            widen_b_v(i, BLOCKS - nv, BLOCKS)
            if i >= PERM_FROM:
                permute_b(i)

        def ret_transposes(i, tag):
            for g in range(G):
                ret_transpose(i, g, tag)

        def ret_codes(i):
            new_ret_q(i)
            for g in range(G):
                ret_quantize(i, g)

        def cost_column(c):
            nc.vector.tensor_copy(out=cost_col[:, 2 * c : 2 * c + 2], in_=cost_ps[c][:])

        load_ret(0)
        load_pos(0, 0)
        load_pos(0, 1)
        load_pos(1, 0)
        load_ret(1)
        load_pos(1, 1)
        load_pos(2, 0)
        load_pos(2, 1)
        load_pos(3, 0)
        load_pos(3, 1)
        load_ret(2)
        load_ret(3)
        load_ret(4)
        load_ret(5)
        load_ret(6)
        load_ret(7)
        widen_b12(0, 0)
        pos_transpose(0, 0, "tp")
        pos_transpose(0, 1, "mx")
        widen_a12(0)
        ret_transposes(0, "tp")
        pos_copies(0, 1)
        pos_magnitudes(0)
        pos_transpose(1, 0, "mx")
        pos_transpose(1, 1, "tp")
        ret_copies(0, 0)
        widen_a12(1)
        ret_codes(0)
        cost_sum(0, "tp")
        pos_codes(0)
        pos_transpose(2, 0, "tp")
        pos_transpose(3, 0, "mx")
        pos_transpose(2, 1, "tp")
        pos_copies(1, 0)
        pos_magnitudes(1)
        widen_b12(1, 0)
        pos_transpose(3, 1, "tp")
        pos_codes(1)
        pos_copies(3, 0)
        cost_sum(1, "mx")
        pos_copies(2, 1)
        ret_transposes(1, "mx")
        cost_column(0)
        product(0, 0, 0)
        ret_copies(1, 0)
        product(0, 1, 0)
        cost_column(1)
        cost_spread_tensor(0, "tp")
        pos_magnitudes(3)
        cost_spread_copy(0)
        pos_codes(2)
        cost_sum(3, "tp")
        pos_magnitudes(2)
        ret_codes(1)
        cost_sum(2, "tp")
        product(1, 0, 0)
        pos_codes(3)
        product(1, 1, 0)
        finish(0, 0, 0)
        cost_column(3)
        product(0, 0, 1)
        finish(0, 1, 0)
        widen_b12(2, 0)
        cost_column(2)
        product(1, 0, 1)
        widen_b12(3, 0)
        cost_spread_tensor(1, "tp")
        widen_a12(2)
        ret_transposes(2, "tp")
        cost_spread_copy(1)
        finish(1, 0, 0)
        widen_a12(3)
        ret_transposes(3, "tp")
        finish(0, 0, 1)
        finish(1, 1, 0)
        ret_copies(2, 0)
        finish(1, 0, 1)
        product(1, 1, 1)
        product(0, 1, 1)
        ret_codes(2)
        widen_b12(4, 0)
        finish(1, 1, 1)
        finish(0, 1, 1)
        ret_copies(3, 0)
        widen_a12(4)

        for i in range(2, PAIRS):
            far = i + 2
            if i + 1 < PAIRS:
                ret_codes(i + 1)
            for s in range(2):
                for h in range(2):
                    if i == PAIRS - 1 and s == 1 and h == 1:
                        for n0 in (0, 256):
                            product(i, s, h, n0, 256)
                            finish(i, s, h, n0, 256)
                    else:
                        product(i, s, h)
                        finish(i, s, h)
            if far < PAIRS:
                ret_transposes(far, "tp")
                if far + 1 < PAIRS:
                    new_wide(far + 1)
                    widen_b(far + 1, 0, 8)
                ret_copies(far, 0)
                if far + 1 < PAIRS:
                    widen_b(far + 1, 8, 12)
                    if far + 1 >= PERM_FROM:
                        permute_b(far + 1)
                    widen_a(far + 1, 0, BLOCKS)
